import numpy as np
import ml_dtypes


def mxq(x, axis, fmt="e4m3"):
    dtype, down = {"e4m3": (ml_dtypes.float8_e4m3fn, 7), "e5m2": (ml_dtypes.float8_e5m2, 14)}[fmt]
    v = np.moveaxis(np.asarray(x, np.float32).astype(ml_dtypes.bfloat16).astype(np.float64), axis, -1)
    blocks = v.reshape(v.shape[:-1] + (-1, 32))
    amax = np.abs(blocks).max(-1, keepdims=True)
    byte = np.maximum(np.where(amax > 0, np.frexp(amax)[1] - 1 + 127, 0) - down, 1)
    scale = np.exp2(byte - 127.0)
    codes = (blocks / scale).astype(np.float32).astype(dtype).astype(np.float64)
    return np.moveaxis((codes * scale).reshape(v.shape), -1, axis)


WIDE = False


def mx_kscale(k):
    if not WIDE:
        return np.ones(k)
    levels = np.array([10, -10, 5, -5, 0])
    if k % 512:
        return np.exp2(np.random.permutation(np.resize(levels, k // 32))).repeat(32)
    a = np.empty((k // 512, 16))
    for p in range(k // 512):
        a[p, :8] = np.random.permutation(np.resize(levels, 8))
        for g in range(8):
            far = levels[np.abs(levels - a[p, g]) >= 10]
            a[p, g + 8] = far[np.random.randint(len(far))]
    return np.exp2(a.ravel()).repeat(32)


def f64(x):
    return np.asarray(x).astype(np.float64)


def striped(idx):
    return np.tile(idx.reshape(-1, 16).T, (8, 1)).astype(np.uint16)


def unstriped(offs):
    return offs[:16].T.reshape(-1).astype(np.int64)


def pack_weight(w):
    k, n = w.shape
    w = f64(np.asarray(w, np.float32).astype(ml_dtypes.bfloat16)).reshape(k // 32, 32, n)
    amax = np.abs(w).max(1)
    byte = np.clip(np.where(amax > 0, np.frexp(amax)[1] - 1 + 127 - 7, 1), 1, 254)
    scaled = (w * np.exp2(127.0 - byte)[:, None, :]).reshape(k, n).astype(np.float32)
    words = np.ascontiguousarray(scaled.reshape(k // 512, 128, 4, n).transpose(0, 1, 3, 2)).astype(ml_dtypes.float8_e4m3fn).view(np.uint8)
    return words, np.ascontiguousarray(byte.astype(np.uint8).reshape(k // 512, 16, n))


def unpack_weight(words, scales):
    g, p, n, _ = words.shape
    vals = np.ascontiguousarray(words).view(ml_dtypes.float8_e4m3fn).astype(np.float64) * np.repeat(np.exp2(scales.astype(np.float64) - 127.0), 8, axis=1)[..., None]
    return vals.transpose(0, 1, 3, 2).reshape(g * 512, n)


def gelu(v):
    return 0.5 * v * (1.0 + np.tanh(np.sqrt(2.0 / np.pi) * (v + 0.044715 * v**3)))


K, T, S, N, H, W, U = 512, 2048, 512, 256, 512, 2048, 1024


def setup_inputs():
    n = np.random.standard_normal
    s = mx_kscale(K)[:, None]
    u = mx_kscale(H)
    packed_xT = pack_weight(n((K, T)) * s)
    packed_eT = pack_weight(n((K, W)) * s)
    return {
        "x_words": packed_xT[0],
        "x_scales": packed_xT[1],
        "w1": (n((K, H)) / np.sqrt(K) / s).astype(np.float32),
        "e_words": packed_eT[0],
        "e_scales": packed_eT[1],
        "w2": (n((K, H)) / np.sqrt(K) / s).astype(np.float32),
        "mod": (np.random.uniform(0.4, 1.6, (H, U))).astype(np.float32),
        "unit": (np.random.uniform(0.6, 1.4, (H, 1)) * u[:, None]).astype(np.float32),
        "w3": (n((H, N)) / np.sqrt(H) / u[:, None]).astype(np.float32),
        "res": (n((N, U))).astype(np.float32),
        "offs": striped(np.random.permutation(T)[:S]),
        "nxt": striped(np.random.permutation(W)[:S]),
        "par": striped(np.random.permutation(np.concatenate([np.arange(S), np.random.randint(0, S, U - S)]))),
    }


def reference(x_words, x_scales, w1, e_words, e_scales, w2, mod, unit, w3, res, offs, nxt, par):
    xq = unpack_weight(x_words, x_scales)[:, unstriped(offs)]
    y = mxq(f64(w1), 0, "e4m3").T @ xq
    e_nxt = unpack_weight(e_words, e_scales)[:, unstriped(nxt)]
    ye = mxq(f64(w2), 0, "e4m3").T @ e_nxt
    jn = gelu(y + ye)
    mu = jn.mean(axis=1, keepdims=True)
    cn = jn - mu
    c2 = (cn) ** 2
    va = c2.mean(axis=1, keepdims=True)
    nr = cn / np.sqrt(va + 0.1)
    vp = nr[:, unstriped(par)]
    hid = f64(unit) * (vp * f64(mod))
    rr = mxq(f64(w3), 0, "e4m3").T @ mxq(hid, 0, "e4m3")
    return f64(res) + rr

@@ -1,0 +1,202 @@
+from contextlib import ExitStack
+
+import concourse.mybir as mybir
+
+K, T, S, N, H, U = 512, 2048, 512, 256, 512, 1024
+FLOPS = 2 * K * H * S * 2 + 2 * H * N * U
+
+F32 = mybir.dt.float32
+BF16 = mybir.dt.bfloat16
+I32 = mybir.dt.int32
+U32 = mybir.dt.uint32
+U16 = mybir.dt.uint16
+U8 = mybir.dt.uint8
+FP8X4 = mybir.dt.float8_e4m3fn_x4
+ALU = mybir.AluOpType
+ACT = mybir.ActivationFunctionType
+
+P = 128
+PACK = 4
+EPS = 0.1
+CHUNKS = [256,256,256,256]
+E_ROW = 4
+BN_TILES = 2
+WIN = 512
+
+
+def tile_picked_ymtph_add_p_kernel(
+    tc, x_words, x_scales, w1, e_words, e_scales, w2, mod, unit, w3, res, offs, nxt, par, out
+):
+    nc = tc.nc
+    with ExitStack() as ctx:
+        keep = ctx.enter_context(tc.tile_pool(name="keep", bufs=1))
+        psum = ctx.enter_context(tc.psum_pool(name="psum", bufs=1))
+
+        def sb(name, shape, dtype):
+            return keep.tile(shape, dtype, name=name, align_bytes=64)
+
+        offs_t = sb("offs_t", [P, S // 16], U16)
+        nxt_t = sb("nxt_t", [P, S // 16], U16)
+        par_t = sb("par_t", [P, U // 16], U16)
+        xw = sb("xw", [P, T], I32)
+        ew = sb("ew", [P, T], I32)
+        xs = sb("xs", [P, T], U8)
+        es = sb("es", [P, T], U8)
+        w1_raw = sb("w1_raw", [P, PACK, H], F32)
+        w2_raw = sb("w2_raw", [P, PACK, H], F32)
+        w3_raw = sb("w3_raw", [P, PACK, N], F32)
+        unit_t = sb("unit_t", [P, PACK], F32)
+        mod_t = [sb("mod%d" % t, [P, U], F32) for t in range(PACK)]
+        res_t = sb("res_t", [P, 2, U], F32)
+        minus_half = sb("minus_half", [P, 1], F32)
+        win = [sb("win%d" % t, [P, WIN], F32) for t in range(PACK)]
+
+        nc.vector.memset(xs[:].bitcast(I32), 0)
+        nc.gpsimd.memset(es[:].bitcast(I32), 0)
+        nc.gpsimd.memset(minus_half[:], -0.5)
+        if WIN > S:
+            for t in range(PACK):
+                nc.gpsimd.memset(win[t][:, S:WIN], 0.0)
+        warm = sb("warm", [P, 1], F32)
+        nc.scalar.activation(out=warm[:], in_=minus_half[:], func=ACT.Gelu_apprx_tanh)
+
+        def load_scale_rows(tile, scales, row0, queue=nc.sync):
+            for q in range(4):
+                queue.dma_start(
+                    out=tile[32 * q + row0 : 32 * q + row0 + 4, :].bitcast(I32),
+                    in_=scales[0, 4 * q : 4 * q + 4, :].bitcast(I32),
+                )
+
+        def words(ap):
+            return ap[0].rearrange("p n t -> p (n t)").bitcast(I32)
+
+        nc.sync.dma_start(out=w1_raw[:, 0:2, :], in_=w1.rearrange("(p j) c -> p j c", j=PACK)[:, 0:2, :])
+        nc.sync.dma_start(offs_t[:], offs)
+        nc.sync.dma_start(nxt_t[:], nxt)
+        nc.sync.dma_start(par_t[:], par)
+        nc.sync.dma_start(out=unit_t[:], in_=unit.rearrange("(p t) o -> p (t o)", t=PACK))
+        nc.sync.dma_start(out=w1_raw[:, 2:4, :], in_=w1.rearrange("(p j) c -> p j c", j=PACK)[:, 2:4, :])
+        nc.sync.dma_start(out=w2_raw[:, 0:2, :], in_=w2.rearrange("(p j) c -> p j c", j=PACK)[:, 0:2, :])
+        nc.sync.dma_start(out=w2_raw[:, 2:4, :], in_=w2.rearrange("(p j) c -> p j c", j=PACK)[:, 2:4, :])
+        load_scale_rows(xs, x_scales, 0)
+        nc.sync.dma_start(out=xw[:], in_=words(x_words))
+        load_scale_rows(es, e_scales, E_ROW)
+        nc.sync.dma_start(out=ew[:], in_=words(e_words))
+        nc.sync.dma_start(out=w3_raw[:], in_=w3.rearrange("(p j) c -> p j c", j=PACK))
+        mod_rows = mod.rearrange("(p t) r -> p t r", t=PACK)
+        for t in range(PACK):
+            nc.sync.dma_start(out=mod_t[t][:], in_=mod_rows[:, t, :])
+        nc.sync.dma_start(out=res_t[:], in_=res.rearrange("(a p) r -> p a r", p=P))
+
+        def quantise(name, grouped, width):
+            codes = sb(name + "_codes", [P, width], U32)
+            scales = sb(name + "_scales", [P, width], U8)
+            nc.vector.quantize_mx(out=codes[:].bitcast(FP8X4), scales=scales[:], in_=grouped[:])
+            return codes, scales
+
+        def dealt(name, raw, copy):
+            grouped = sb(name + "_bf16", [P, H * PACK], BF16)
+            copy(
+                out=grouped[:].rearrange("p (t m j) -> p m t j", t=PACK, j=PACK),
+                in_=raw[:].rearrange("p j (m t) -> p m t j", t=PACK),
+            )
+            return quantise(name, grouped, H)
+
+        def pick(name, table, offsets, dtype):
+            picked = sb(name, [P, S], dtype)
+            nc.vector.tensor_copy(picked[:], table.indirect(offsets[:]))
+            return picked
+
+        w1c, w1s = dealt("w1", w1_raw, nc.vector.tensor_copy)
+        xs_g = pick("xs_g", xs[:], offs_t, U8)
+        es_g = pick("es_g", es[:], nxt_t, U8)
+        w2c, w2s = dealt("w2", w2_raw, nc.scalar.copy)
+        xw_g = pick("xw_g", xw[:].bitcast(U32), offs_t, U32)
+        pre = [psum.tile([P, S], F32, name="pre%d" % t) for t in range(PACK)]
+        for t in range(PACK):
+            cols = slice(P * t, P * (t + 1))
+            nc.tensor.matmul_mx(
+                out=pre[t][:], lhsT=w1c[:, cols].bitcast(FP8X4), lhsT_scale=w1s[:, cols],
+                rhs=xw_g[:].bitcast(FP8X4), rhs_scale=xs_g[:], start=True, stop=False,
+            )
+        ew_g = pick("ew_g", ew[:].bitcast(U32), nxt_t, U32)
+        for t in range(PACK):
+            cols = slice(P * t, P * (t + 1))
+            nc.tensor.matmul_mx(
+                out=pre[t][:], lhsT=w2c[:, cols].bitcast(FP8X4), lhsT_scale=w2s[:, cols],
+                rhs=ew_g[:].bitcast(FP8X4), rhs_scale=es_g[E_ROW:P, :], start=False, stop=True,
+            )
+
+        w3_bf16 = sb("w3_bf16", [P, N * PACK], BF16)
+        nc.vector.tensor_copy(
+            out=w3_bf16[:].rearrange("p (c i j) -> p c j i", i=4, j=PACK),
+            in_=w3_raw[:].rearrange("p j (c i) -> p c j i", i=4),
+        )
+        w3c, w3s = quantise("w3", w3_bf16, N)
+
+        jn = [sb("jn%d" % t, [P, S], F32) for t in range(PACK)]
+        squares = sb("squares", [P, S], BF16)
+        coef = []
+        for t in range(PACK):
+            var_eps = sb("var_eps%d" % t, [P, 1], F32)
+            rstd = sb("rstd%d" % t, [P, 1], F32)
+            gain = sb("gain%d" % t, [P, 1], F32)
+            shift = sb("shift%d" % t, [P, 1], F32)
+            if t < BN_TILES:
+                stats = sb("stats%d" % t, [P, 6], F32)
+                mv = sb("mv%d" % t, [P, 2], F32)
+                nc.scalar.activation(out=jn[t][:], in_=pre[t][:], func=ACT.Gelu_apprx_tanh)
+                nc.vector.bn_stats(out=stats[:], in_=jn[t][:])
+                nc.vector.bn_aggr(out=mv[:], in_=stats[:])
+                total, to_mean, spread, to_var = mv[:, 0:1], 1.0, mv[:, 1:2], 1.0
+            else:
+                row_sum = sb("row_sum%d" % t, [P, 1], F32)
+                row_sq = sb("row_sq%d" % t, [P, 1], F32)
+                nc.scalar.activation(out=jn[t][:], in_=pre[t][:], func=ACT.Gelu_apprx_tanh, accum_out=row_sum[:])
+                nc.scalar.activation(
+                    out=squares[:], in_=jn[t][:], func=ACT.Square, scale=-float(S), bias=row_sum[:], accum_out=row_sq[:]
+                )
+                total, to_mean, spread, to_var = row_sum[:], 1.0 / S, row_sq[:], 1.0 / S**3
+            nc.gpsimd.tensor_scalar(out=var_eps[:], in0=spread, scalar1=to_var, scalar2=EPS, op0=ALU.mult, op1=ALU.add)
+            nc.gpsimd.tensor_tensor(out=rstd[:], in0=var_eps[:], in1=minus_half[:], op=ALU.pow)
+            nc.gpsimd.tensor_tensor(out=gain[:], in0=rstd[:], in1=unit_t[:, t : t + 1], op=ALU.mult)
+            nc.gpsimd.tensor_scalar(out=shift[:], in0=total, scalar1=gain[:], scalar2=-to_mean, op0=ALU.mult, op1=ALU.mult)
+            coef.append((gain, shift))
+        for t in range(PACK):
+            gain, shift = coef[t]
+            if t < 1:
+                nc.vector.tensor_scalar(
+                    out=win[t][:, 0:S], in0=jn[t][:], scalar1=gain[:], scalar2=shift[:], op0=ALU.mult, op1=ALU.add
+                )
+            else:
+                nc.scalar.activation(out=win[t][:, 0:S], in_=jn[t][:], func=ACT.Identity, scale=gain[:], bias=shift[:])
+
+        out_rows = out.rearrange("(a p) r -> p a r", p=P)
+        r0 = 0
+        for c, n in enumerate(CHUNKS):
+            cols = slice(r0, r0 + n)
+            prod = sb("prod%d" % c, [P, PACK, n], F32)
+            for t in range(PACK):
+                nc.vector.tensor_tensor(
+                    prod[:, t, :], win[t][:].indirect(par_t[:, r0 // 16 : (r0 + n) // 16]), mod_t[t][:, cols], ALU.mult
+                )
+            hid = sb("hid%d" % c, [P, n * PACK], BF16)
+            nc.scalar.copy(
+                out=hid[:].rearrange("p (g i t) -> p g t i", i=4, t=PACK),
+                in_=prod[:].rearrange("p t (g i) -> p g t i", i=4),
+            )
+            hc, hs = quantise("hid%d" % c, hid, n)
+            result = sb("result%d" % c, [P, 2, n], F32)
+            group = max(1, 512 // (n * 2)) * 2 if n <= 256 else 1
+            for a0 in range(0, 2, min(group, 2)):
+                na = min(group, 2)
+                acc = psum.tile([P, na, n], F32, name="acc", tag="acc", bufs=4)
+                for a in range(a0, a0 + na):
+                    mcols = slice(P * a, P * (a + 1))
+                    nc.tensor.matmul_mx(
+                        out=acc[:, a - a0, :], lhsT=w3c[:, mcols].bitcast(FP8X4), lhsT_scale=w3s[:, mcols],
+                        rhs=hc[:].bitcast(FP8X4), rhs_scale=hs[:], start=True, stop=True,
+                    )
+                nc.vector.tensor_tensor(result[:, a0 : a0 + na, :], acc[:], res_t[:, a0 : a0 + na, cols], ALU.add)
+            nc.sync.dma_start(out=out_rows[:, :, cols], in_=result[:])
+            r0 += n

@@ -20,6 +20,9 @@ PACK = 4
 EPS = 0.1
 CHUNKS = [256,256,256,256]
 E_ROW = 4
+LAG = 1
+EARLY = 2
+PIECE = 256
 BN_TILES = 2
 WIN = 512
 
@@ -32,8 +35,8 @@ def tile_picked_ymtph_add_p_kernel(
         keep = ctx.enter_context(tc.tile_pool(name="keep", bufs=1))
         psum = ctx.enter_context(tc.psum_pool(name="psum", bufs=1))
 
-        def sb(name, shape, dtype):
-            return keep.tile(shape, dtype, name=name, align_bytes=64)
+        def sb(name, shape, dtype, slot=None, bufs=1):
+            return keep.tile(shape, dtype, name=name, tag=slot or name, bufs=bufs, align_bytes=64)
 
         offs_t = sb("offs_t", [P, S // 16], U16)
         nxt_t = sb("nxt_t", [P, S // 16], U16)
@@ -49,22 +52,22 @@ def tile_picked_ymtph_add_p_kernel(
         mod_t = [sb("mod%d" % t, [P, U], F32) for t in range(PACK)]
         res_t = sb("res_t", [P, 2, U], F32)
         minus_half = sb("minus_half", [P, 1], F32)
-        win = [sb("win%d" % t, [P, WIN], F32) for t in range(PACK)]
+        win = [sb("win%d" % t, [P, WIN if t < EARLY else S], F32) for t in range(PACK)]
 
         nc.vector.memset(xs[:].bitcast(I32), 0)
-        nc.gpsimd.memset(es[:].bitcast(I32), 0)
-        nc.gpsimd.memset(minus_half[:], -0.5)
+        nc.vector.memset(es[:].bitcast(I32), 0)
+        nc.vector.memset(minus_half[:], -0.5)
         if WIN > S:
-            for t in range(PACK):
-                nc.gpsimd.memset(win[t][:, S:WIN], 0.0)
+            for t in range(EARLY):
+                nc.vector.memset(win[t][:, S:WIN], 0.0)
         warm = sb("warm", [P, 1], F32)
         nc.scalar.activation(out=warm[:], in_=minus_half[:], func=ACT.Gelu_apprx_tanh)
 
         def load_scale_rows(tile, scales, row0, queue=nc.sync):
-            for q in range(4):
+            for r in range(4):
                 queue.dma_start(
-                    out=tile[32 * q + row0 : 32 * q + row0 + 4, :].bitcast(I32),
-                    in_=scales[0, 4 * q : 4 * q + 4, :].bitcast(I32),
+                    out=tile[row0 + r : P : 32, :].bitcast(I32),
+                    in_=scales[0, r:16:4, :].bitcast(I32),
                 )
 
         def words(ap):
@@ -76,10 +79,10 @@ def tile_picked_ymtph_add_p_kernel(
         nc.sync.dma_start(par_t[:], par)
         nc.sync.dma_start(out=unit_t[:], in_=unit.rearrange("(p t) o -> p (t o)", t=PACK))
         nc.sync.dma_start(out=w1_raw[:, 2:4, :], in_=w1.rearrange("(p j) c -> p j c", j=PACK)[:, 2:4, :])
-        nc.sync.dma_start(out=w2_raw[:, 0:2, :], in_=w2.rearrange("(p j) c -> p j c", j=PACK)[:, 0:2, :])
-        nc.sync.dma_start(out=w2_raw[:, 2:4, :], in_=w2.rearrange("(p j) c -> p j c", j=PACK)[:, 2:4, :])
+        nc.sync.dma_start(out=xw[:, 0 : T // 2], in_=words(x_words)[:, 0 : T // 2])
+        nc.sync.dma_start(out=xw[:, T // 2 : T], in_=words(x_words)[:, T // 2 : T])
         load_scale_rows(xs, x_scales, 0)
-        nc.sync.dma_start(out=xw[:], in_=words(x_words))
+        nc.sync.dma_start(out=w2_raw[:], in_=w2.rearrange("(p j) c -> p j c", j=PACK))
         load_scale_rows(es, e_scales, E_ROW)
         nc.sync.dma_start(out=ew[:], in_=words(e_words))
         nc.sync.dma_start(out=w3_raw[:], in_=w3.rearrange("(p j) c -> p j c", j=PACK))
@@ -88,30 +91,31 @@ def tile_picked_ymtph_add_p_kernel(
             nc.sync.dma_start(out=mod_t[t][:], in_=mod_rows[:, t, :])
         nc.sync.dma_start(out=res_t[:], in_=res.rearrange("(a p) r -> p a r", p=P))
 
-        def quantise(name, grouped, width):
-            codes = sb(name + "_codes", [P, width], U32)
+        def quantise(name, grouped, width, slot=None, bufs=1):
+            codes = sb(name + "_codes", [P, width], U32, slot, bufs)
             scales = sb(name + "_scales", [P, width], U8)
             nc.vector.quantize_mx(out=codes[:].bitcast(FP8X4), scales=scales[:], in_=grouped[:])
             return codes, scales
 
-        def dealt(name, raw, copy):
-            grouped = sb(name + "_bf16", [P, H * PACK], BF16)
-            copy(
-                out=grouped[:].rearrange("p (t m j) -> p m t j", t=PACK, j=PACK),
-                in_=raw[:].rearrange("p j (m t) -> p m t j", t=PACK),
-            )
-            return quantise(name, grouped, H)
+        def dealt(name, raw, split, slot=None, code_slot=None):
+            grouped = sb(name + "_bf16", [P, H * PACK], BF16, slot)
+            dst = grouped[:].rearrange("p (t m j) -> p m t j", t=PACK, j=PACK)
+            src = raw[:].rearrange("p j (m t) -> p m t j", t=PACK)
+            if split > 0:
+                nc.vector.tensor_copy(out=dst[:, 0:split], in_=src[:, 0:split])
+            if split < P:
+                nc.scalar.copy(out=dst[:, split:P], in_=src[:, split:P])
+            return quantise(name, grouped, H, code_slot)
 
-        def pick(name, table, offsets, dtype):
-            picked = sb(name, [P, S], dtype)
+        def pick(name, table, offsets, dtype, slot=None):
+            picked = sb(name, [P, S], dtype, slot)
             nc.vector.tensor_copy(picked[:], table.indirect(offsets[:]))
             return picked
 
-        w1c, w1s = dealt("w1", w1_raw, nc.vector.tensor_copy)
-        xs_g = pick("xs_g", xs[:], offs_t, U8)
-        es_g = pick("es_g", es[:], nxt_t, U8)
-        w2c, w2s = dealt("w2", w2_raw, nc.scalar.copy)
+        w1c, w1s = dealt("w1", w1_raw, 128)
         xw_g = pick("xw_g", xw[:].bitcast(U32), offs_t, U32)
+        xs_g = pick("xs_g", xs[:], offs_t, U8, "xw")
+        es_g = pick("es_g", es[:], nxt_t, U8)
         pre = [psum.tile([P, S], F32, name="pre%d" % t) for t in range(PACK)]
         for t in range(PACK):
             cols = slice(P * t, P * (t + 1))
@@ -119,6 +123,7 @@ def tile_picked_ymtph_add_p_kernel(
                 out=pre[t][:], lhsT=w1c[:, cols].bitcast(FP8X4), lhsT_scale=w1s[:, cols],
                 rhs=xw_g[:].bitcast(FP8X4), rhs_scale=xs_g[:], start=True, stop=False,
             )
+        w2c, w2s = dealt("w2", w2_raw, 56, "xs", "es")
         ew_g = pick("ew_g", ew[:].bitcast(U32), nxt_t, U32)
         for t in range(PACK):
             cols = slice(P * t, P * (t + 1))
@@ -127,76 +132,95 @@ def tile_picked_ymtph_add_p_kernel(
                 rhs=ew_g[:].bitcast(FP8X4), rhs_scale=es_g[E_ROW:P, :], start=False, stop=True,
             )
 
-        w3_bf16 = sb("w3_bf16", [P, N * PACK], BF16)
+        w3_bf16 = sb("w3_bf16", [P, N * PACK], BF16, "ew")
         nc.vector.tensor_copy(
-            out=w3_bf16[:].rearrange("p (c i j) -> p c j i", i=4, j=PACK),
-            in_=w3_raw[:].rearrange("p j (c i) -> p c j i", i=4),
+            out=w3_bf16[:].rearrange("p (c i j) -> p c j i", i=2, j=PACK),
+            in_=w3_raw[:].rearrange("p j (c i) -> p c j i", i=2),
         )
         w3c, w3s = quantise("w3", w3_bf16, N)
 
         jn = [sb("jn%d" % t, [P, S], F32) for t in range(PACK)]
+        unit_mean = sb("unit_mean", [P, PACK - EARLY], F32)
+        nc.vector.tensor_scalar_mul(out=unit_mean[:], in0=unit_t[:, EARLY:PACK], scalar1=-1.0 / S)
+        moments = sb("moments", [P, EARLY, 2], F32)
+        spread = sb("spread", [P, PACK], F32)
         squares = sb("squares", [P, S], BF16)
-        coef = []
+        factors = sb("factors", [P, PACK - EARLY, 2], F32)
+        nc.vector.tensor_copy(out=factors[:, :, 0], in_=unit_t[:, EARLY:PACK])
         for t in range(PACK):
-            var_eps = sb("var_eps%d" % t, [P, 1], F32)
-            rstd = sb("rstd%d" % t, [P, 1], F32)
-            gain = sb("gain%d" % t, [P, 1], F32)
-            shift = sb("shift%d" % t, [P, 1], F32)
-            if t < BN_TILES:
+            if t < EARLY:
                 stats = sb("stats%d" % t, [P, 6], F32)
-                mv = sb("mv%d" % t, [P, 2], F32)
                 nc.scalar.activation(out=jn[t][:], in_=pre[t][:], func=ACT.Gelu_apprx_tanh)
                 nc.vector.bn_stats(out=stats[:], in_=jn[t][:])
-                nc.vector.bn_aggr(out=mv[:], in_=stats[:])
-                total, to_mean, spread, to_var = mv[:, 0:1], 1.0, mv[:, 1:2], 1.0
+                nc.vector.bn_aggr(out=moments[:, t, :], in_=stats[:])
+                nc.vector.tensor_scalar(
+                    out=win[t][:, 0:S], in0=jn[t][:], scalar1=moments[:, t, 0:1], scalar2=unit_t[:, t : t + 1],
+                    op0=ALU.subtract, op1=ALU.mult,
+                )
             else:
                 row_sum = sb("row_sum%d" % t, [P, 1], F32)
-                row_sq = sb("row_sq%d" % t, [P, 1], F32)
                 nc.scalar.activation(out=jn[t][:], in_=pre[t][:], func=ACT.Gelu_apprx_tanh, accum_out=row_sum[:])
                 nc.scalar.activation(
-                    out=squares[:], in_=jn[t][:], func=ACT.Square, scale=-float(S), bias=row_sum[:], accum_out=row_sq[:]
+                    out=squares[:], in_=jn[t][:], func=ACT.Square, scale=-float(S), bias=row_sum[:],
+                    accum_out=spread[:, t : t + 1],
                 )
-                total, to_mean, spread, to_var = row_sum[:], 1.0 / S, row_sq[:], 1.0 / S**3
-            nc.gpsimd.tensor_scalar(out=var_eps[:], in0=spread, scalar1=to_var, scalar2=EPS, op0=ALU.mult, op1=ALU.add)
-            nc.gpsimd.tensor_tensor(out=rstd[:], in0=var_eps[:], in1=minus_half[:], op=ALU.pow)
-            nc.gpsimd.tensor_tensor(out=gain[:], in0=rstd[:], in1=unit_t[:, t : t + 1], op=ALU.mult)
-            nc.gpsimd.tensor_scalar(out=shift[:], in0=total, scalar1=gain[:], scalar2=-to_mean, op0=ALU.mult, op1=ALU.mult)
-            coef.append((gain, shift))
-        for t in range(PACK):
-            gain, shift = coef[t]
-            if t < 1:
-                nc.vector.tensor_scalar(
-                    out=win[t][:, 0:S], in0=jn[t][:], scalar1=gain[:], scalar2=shift[:], op0=ALU.mult, op1=ALU.add
+                nc.scalar.activation(
+                    out=factors[:, t - EARLY, 1:2], in_=row_sum[:], func=ACT.Copy,
+                    scale=unit_mean[:, t - EARLY : t - EARLY + 1],
                 )
-            else:
-                nc.scalar.activation(out=win[t][:, 0:S], in_=jn[t][:], func=ACT.Identity, scale=gain[:], bias=shift[:])
+        nc.vector.tensor_scalar_mul(out=spread[:, 0:EARLY], in0=moments[:, :, 1], scalar1=float(S) ** 3)
+        rstd = sb("rstd", [P, PACK], F32)
+        nc.scalar.activation(out=rstd[:], in_=spread[:], func=ACT.Abs_reciprocal_sqrt, scale=1.0 / S**3, bias=EPS)
+        early = [sb("early%d" % t, [P, U], F32) for t in range(EARLY)]
+        for t in range(EARLY):
+            for r0 in range(0, U, PIECE):
+                r1 = min(U, r0 + PIECE)
+                nc.vector.tensor_tensor(
+                    early[t][:, r0:r1], win[t][:].indirect(par_t[:, r0 // 16 : r1 // 16]), mod_t[t][:, r0:r1], ALU.mult
+                )
+        for t in range(EARLY, PACK):
+            line = sb("line%d" % t, [P, 2], F32)
+            nc.scalar.activation(out=line[:], in_=factors[:, t - EARLY, :], func=ACT.Copy, scale=rstd[:, t : t + 1])
+            nc.scalar.activation(out=win[t][:], in_=jn[t][:], func=ACT.Identity, scale=line[:, 0:1], bias=line[:, 1:2])
 
         out_rows = out.rearrange("(a p) r -> p a r", p=P)
-        r0 = 0
-        for c, n in enumerate(CHUNKS):
+        starts = [sum(CHUNKS[:c]) for c in range(len(CHUNKS))]
+
+        def project(c):
+            r0, n = starts[c], CHUNKS[c]
             cols = slice(r0, r0 + n)
             prod = sb("prod%d" % c, [P, PACK, n], F32)
-            for t in range(PACK):
+            for t in range(EARLY):
+                nc.scalar.activation(out=prod[:, t, :], in_=early[t][:, cols], func=ACT.Copy, scale=rstd[:, t : t + 1])
+            for t in range(EARLY, PACK):
                 nc.vector.tensor_tensor(
                     prod[:, t, :], win[t][:].indirect(par_t[:, r0 // 16 : (r0 + n) // 16]), mod_t[t][:, cols], ALU.mult
                 )
             hid = sb("hid%d" % c, [P, n * PACK], BF16)
             nc.scalar.copy(
-                out=hid[:].rearrange("p (g i t) -> p g t i", i=4, t=PACK),
-                in_=prod[:].rearrange("p t (g i) -> p g t i", i=4),
+                out=hid[:].rearrange("p (g i t) -> p g t i", i=2, t=PACK),
+                in_=prod[:].rearrange("p t (g i) -> p g t i", i=2),
             )
             hc, hs = quantise("hid%d" % c, hid, n)
-            result = sb("result%d" % c, [P, 2, n], F32)
-            group = max(1, 512 // (n * 2)) * 2 if n <= 256 else 1
-            for a0 in range(0, 2, min(group, 2)):
-                na = min(group, 2)
-                acc = psum.tile([P, na, n], F32, name="acc", tag="acc", bufs=4)
-                for a in range(a0, a0 + na):
-                    mcols = slice(P * a, P * (a + 1))
-                    nc.tensor.matmul_mx(
-                        out=acc[:, a - a0, :], lhsT=w3c[:, mcols].bitcast(FP8X4), lhsT_scale=w3s[:, mcols],
-                        rhs=hc[:].bitcast(FP8X4), rhs_scale=hs[:], start=True, stop=True,
-                    )
-                nc.vector.tensor_tensor(result[:, a0 : a0 + na, :], acc[:], res_t[:, a0 : a0 + na, cols], ALU.add)
+            acc = psum.tile([P, 2, n], F32, name="acc%d" % c, tag="acc", bufs=4)
+            for a in range(2):
+                mcols = slice(P * a, P * (a + 1))
+                nc.tensor.matmul_mx(
+                    out=acc[:, a, :], lhsT=w3c[:, mcols].bitcast(FP8X4), lhsT_scale=w3s[:, mcols],
+                    rhs=hc[:].bitcast(FP8X4), rhs_scale=hs[:], start=True, stop=True,
+                )
+            return acc
+
+        def finish(c, acc):
+            cols = slice(starts[c], starts[c] + CHUNKS[c])
+            slot = "hid%d" % (c + LAG) if c + LAG < len(CHUNKS) else None
+            result = sb("result%d" % c, [P, 2, CHUNKS[c]], F32, slot)
+            nc.vector.tensor_tensor(result[:], acc[:], res_t[:, :, cols], ALU.add)
             nc.sync.dma_start(out=out_rows[:, :, cols], in_=result[:])
-            r0 += n
+
+        accs = []
+        for c in range(len(CHUNKS) + LAG):
+            if c < len(CHUNKS):
+                accs.append(project(c))
+            if c >= LAG:
+                finish(c - LAG, accs[c - LAG])

from contextlib import ExitStack

import concourse.mybir as mybir

K, T, S, N, H, U = 512, 2048, 512, 256, 512, 1024
FLOPS = 2 * K * H * S * 2 + 2 * H * N * U

F32 = mybir.dt.float32
BF16 = mybir.dt.bfloat16
I32 = mybir.dt.int32
U32 = mybir.dt.uint32
U16 = mybir.dt.uint16
U8 = mybir.dt.uint8
FP8X4 = mybir.dt.float8_e4m3fn_x4
ALU = mybir.AluOpType
ACT = mybir.ActivationFunctionType

P = 128
PACK = 4
EPS = 0.1
CHUNKS = [256,256,256,256]
E_ROW = 4
LAG = 1
EARLY = 2
PIECE = 256
BN_TILES = 2
WIN = 512


def tile_picked_ymtph_add_p_kernel(
    tc, x_words, x_scales, w1, e_words, e_scales, w2, mod, unit, w3, res, offs, nxt, par, out
):
    nc = tc.nc
    with ExitStack() as ctx:
        keep = ctx.enter_context(tc.tile_pool(name="keep", bufs=1))
        psum = ctx.enter_context(tc.psum_pool(name="psum", bufs=1))

        def sb(name, shape, dtype, slot=None, bufs=1):
            return keep.tile(shape, dtype, name=name, tag=slot or name, bufs=bufs, align_bytes=64)

        offs_t = sb("offs_t", [P, S // 16], U16)
        nxt_t = sb("nxt_t", [P, S // 16], U16)
        par_t = sb("par_t", [P, U // 16], U16)
        xw = sb("xw", [P, T], I32)
        ew = sb("ew", [P, T], I32)
        xs = sb("xs", [P, T], U8)
        es = sb("es", [P, T], U8)
        w1_raw = sb("w1_raw", [P, PACK, H], F32)
        w2_raw = sb("w2_raw", [P, PACK, H], F32)
        w3_raw = sb("w3_raw", [P, PACK, N], F32)
        unit_t = sb("unit_t", [P, PACK], F32)
        mod_t = [sb("mod%d" % t, [P, U], F32) for t in range(PACK)]
        res_t = sb("res_t", [P, 2, U], F32)
        minus_half = sb("minus_half", [P, 1], F32)
        win = [sb("win%d" % t, [P, WIN if t < EARLY else S], F32) for t in range(PACK)]

        nc.vector.memset(xs[:].bitcast(I32), 0)
        nc.vector.memset(es[:].bitcast(I32), 0)
        nc.vector.memset(minus_half[:], -0.5)
        if WIN > S:
            for t in range(EARLY):
                nc.vector.memset(win[t][:, S:WIN], 0.0)
        warm = sb("warm", [P, 1], F32)
        nc.scalar.activation(out=warm[:], in_=minus_half[:], func=ACT.Gelu_apprx_tanh)

        def load_scale_rows(tile, scales, row0, queue=nc.sync):
            for r in range(4):
                queue.dma_start(
                    out=tile[row0 + r : P : 32, :].bitcast(I32),
                    in_=scales[0, r:16:4, :].bitcast(I32),
                )

        def words(ap):
            return ap[0].rearrange("p n t -> p (n t)").bitcast(I32)

        nc.sync.dma_start(out=w1_raw[:, 0:2, :], in_=w1.rearrange("(p j) c -> p j c", j=PACK)[:, 0:2, :])
        nc.sync.dma_start(offs_t[:], offs)
        nc.sync.dma_start(nxt_t[:], nxt)
        nc.sync.dma_start(par_t[:], par)
        nc.sync.dma_start(out=unit_t[:], in_=unit.rearrange("(p t) o -> p (t o)", t=PACK))
        nc.sync.dma_start(out=w1_raw[:, 2:4, :], in_=w1.rearrange("(p j) c -> p j c", j=PACK)[:, 2:4, :])
        nc.sync.dma_start(out=xw[:, 0 : T // 2], in_=words(x_words)[:, 0 : T // 2])
        nc.sync.dma_start(out=xw[:, T // 2 : T], in_=words(x_words)[:, T // 2 : T])
        load_scale_rows(xs, x_scales, 0)
        nc.sync.dma_start(out=w2_raw[:], in_=w2.rearrange("(p j) c -> p j c", j=PACK))
        load_scale_rows(es, e_scales, E_ROW)
        nc.sync.dma_start(out=ew[:], in_=words(e_words))
        nc.sync.dma_start(out=w3_raw[:], in_=w3.rearrange("(p j) c -> p j c", j=PACK))
        mod_rows = mod.rearrange("(p t) r -> p t r", t=PACK)
        for t in range(PACK):
            nc.sync.dma_start(out=mod_t[t][:], in_=mod_rows[:, t, :])
        nc.sync.dma_start(out=res_t[:], in_=res.rearrange("(a p) r -> p a r", p=P))

        def quantise(name, grouped, width, slot=None, bufs=1):
            codes = sb(name + "_codes", [P, width], U32, slot, bufs)
            scales = sb(name + "_scales", [P, width], U8)
            nc.vector.quantize_mx(out=codes[:].bitcast(FP8X4), scales=scales[:], in_=grouped[:])
            return codes, scales

        def dealt(name, raw, split, slot=None, code_slot=None):
            grouped = sb(name + "_bf16", [P, H * PACK], BF16, slot)
            dst = grouped[:].rearrange("p (t m j) -> p m t j", t=PACK, j=PACK)
            src = raw[:].rearrange("p j (m t) -> p m t j", t=PACK)
            if split > 0:
                nc.vector.tensor_copy(out=dst[:, 0:split], in_=src[:, 0:split])
            if split < P:
                nc.scalar.copy(out=dst[:, split:P], in_=src[:, split:P])
            return quantise(name, grouped, H, code_slot)

        def pick(name, table, offsets, dtype, slot=None):
            picked = sb(name, [P, S], dtype, slot)
            nc.vector.tensor_copy(picked[:], table.indirect(offsets[:]))
            return picked

        w1c, w1s = dealt("w1", w1_raw, 128)
        xw_g = pick("xw_g", xw[:].bitcast(U32), offs_t, U32)
        xs_g = pick("xs_g", xs[:], offs_t, U8, "xw")
        es_g = pick("es_g", es[:], nxt_t, U8)
        pre = [psum.tile([P, S], F32, name="pre%d" % t) for t in range(PACK)]
        for t in range(PACK):
            cols = slice(P * t, P * (t + 1))
            nc.tensor.matmul_mx(
                out=pre[t][:], lhsT=w1c[:, cols].bitcast(FP8X4), lhsT_scale=w1s[:, cols],
                rhs=xw_g[:].bitcast(FP8X4), rhs_scale=xs_g[:], start=True, stop=False,
            )
        w2c, w2s = dealt("w2", w2_raw, 56, "xs", "es")
        ew_g = pick("ew_g", ew[:].bitcast(U32), nxt_t, U32)
        for t in range(PACK):
            cols = slice(P * t, P * (t + 1))
            nc.tensor.matmul_mx(
                out=pre[t][:], lhsT=w2c[:, cols].bitcast(FP8X4), lhsT_scale=w2s[:, cols],
                rhs=ew_g[:].bitcast(FP8X4), rhs_scale=es_g[E_ROW:P, :], start=False, stop=True,
            )

        w3_bf16 = sb("w3_bf16", [P, N * PACK], BF16, "ew")
        nc.vector.tensor_copy(
            out=w3_bf16[:].rearrange("p (c i j) -> p c j i", i=2, j=PACK),
            in_=w3_raw[:].rearrange("p j (c i) -> p c j i", i=2),
        )
        w3c, w3s = quantise("w3", w3_bf16, N)

        jn = [sb("jn%d" % t, [P, S], F32) for t in range(PACK)]
        unit_mean = sb("unit_mean", [P, PACK - EARLY], F32)
        nc.vector.tensor_scalar_mul(out=unit_mean[:], in0=unit_t[:, EARLY:PACK], scalar1=-1.0 / S)
        moments = sb("moments", [P, EARLY, 2], F32)
        spread = sb("spread", [P, PACK], F32)
        squares = sb("squares", [P, S], BF16)
        factors = sb("factors", [P, PACK - EARLY, 2], F32)
        nc.vector.tensor_copy(out=factors[:, :, 0], in_=unit_t[:, EARLY:PACK])
        for t in range(PACK):
            if t < EARLY:
                stats = sb("stats%d" % t, [P, 6], F32)
                nc.scalar.activation(out=jn[t][:], in_=pre[t][:], func=ACT.Gelu_apprx_tanh)
                nc.vector.bn_stats(out=stats[:], in_=jn[t][:])
                nc.vector.bn_aggr(out=moments[:, t, :], in_=stats[:])
                nc.vector.tensor_scalar(
                    out=win[t][:, 0:S], in0=jn[t][:], scalar1=moments[:, t, 0:1], scalar2=unit_t[:, t : t + 1],
                    op0=ALU.subtract, op1=ALU.mult,
                )
            else:
                row_sum = sb("row_sum%d" % t, [P, 1], F32)
                nc.scalar.activation(out=jn[t][:], in_=pre[t][:], func=ACT.Gelu_apprx_tanh, accum_out=row_sum[:])
                nc.scalar.activation(
                    out=squares[:], in_=jn[t][:], func=ACT.Square, scale=-float(S), bias=row_sum[:],
                    accum_out=spread[:, t : t + 1],
                )
                nc.scalar.activation(
                    out=factors[:, t - EARLY, 1:2], in_=row_sum[:], func=ACT.Copy,
                    scale=unit_mean[:, t - EARLY : t - EARLY + 1],
                )
        nc.vector.tensor_scalar_mul(out=spread[:, 0:EARLY], in0=moments[:, :, 1], scalar1=float(S) ** 3)
        rstd = sb("rstd", [P, PACK], F32)
        nc.scalar.activation(out=rstd[:], in_=spread[:], func=ACT.Abs_reciprocal_sqrt, scale=1.0 / S**3, bias=EPS)
        early = [sb("early%d" % t, [P, U], F32) for t in range(EARLY)]
        for t in range(EARLY):
            for r0 in range(0, U, PIECE):
                r1 = min(U, r0 + PIECE)
                nc.vector.tensor_tensor(
                    early[t][:, r0:r1], win[t][:].indirect(par_t[:, r0 // 16 : r1 // 16]), mod_t[t][:, r0:r1], ALU.mult
                )
        for t in range(EARLY, PACK):
            line = sb("line%d" % t, [P, 2], F32)
            nc.scalar.activation(out=line[:], in_=factors[:, t - EARLY, :], func=ACT.Copy, scale=rstd[:, t : t + 1])
            nc.scalar.activation(out=win[t][:], in_=jn[t][:], func=ACT.Identity, scale=line[:, 0:1], bias=line[:, 1:2])

        out_rows = out.rearrange("(a p) r -> p a r", p=P)
        starts = [sum(CHUNKS[:c]) for c in range(len(CHUNKS))]

        def project(c):
            r0, n = starts[c], CHUNKS[c]
            cols = slice(r0, r0 + n)
            prod = sb("prod%d" % c, [P, PACK, n], F32)
            for t in range(EARLY):
                nc.scalar.activation(out=prod[:, t, :], in_=early[t][:, cols], func=ACT.Copy, scale=rstd[:, t : t + 1])
            for t in range(EARLY, PACK):
                nc.vector.tensor_tensor(
                    prod[:, t, :], win[t][:].indirect(par_t[:, r0 // 16 : (r0 + n) // 16]), mod_t[t][:, cols], ALU.mult
                )
            hid = sb("hid%d" % c, [P, n * PACK], BF16)
            nc.scalar.copy(
                out=hid[:].rearrange("p (g i t) -> p g t i", i=2, t=PACK),
                in_=prod[:].rearrange("p t (g i) -> p g t i", i=2),
            )
            hc, hs = quantise("hid%d" % c, hid, n)
            acc = psum.tile([P, 2, n], F32, name="acc%d" % c, tag="acc", bufs=4)
            for a in range(2):
                mcols = slice(P * a, P * (a + 1))
                nc.tensor.matmul_mx(
                    out=acc[:, a, :], lhsT=w3c[:, mcols].bitcast(FP8X4), lhsT_scale=w3s[:, mcols],
                    rhs=hc[:].bitcast(FP8X4), rhs_scale=hs[:], start=True, stop=True,
                )
            return acc

        def finish(c, acc):
            cols = slice(starts[c], starts[c] + CHUNKS[c])
            slot = "hid%d" % (c + LAG) if c + LAG < len(CHUNKS) else None
            result = sb("result%d" % c, [P, 2, CHUNKS[c]], F32, slot)
            nc.vector.tensor_tensor(result[:], acc[:], res_t[:, :, cols], ALU.add)
            nc.sync.dma_start(out=out_rows[:, :, cols], in_=result[:])

        accs = []
        for c in range(len(CHUNKS) + LAG):
            if c < len(CHUNKS):
                accs.append(project(c))
            if c >= LAG:
                finish(c - LAG, accs[c - LAG])
